import numpy as np
import ml_dtypes


def mxq(x, axis, fmt="e4m3"):
    dtype, down = {"e4m3": (ml_dtypes.float8_e4m3fn, 7), "e5m2": (ml_dtypes.float8_e5m2, 14)}[fmt]
    v = np.moveaxis(np.asarray(x, np.float32).astype(ml_dtypes.bfloat16).astype(np.float64), axis, -1)
    blocks = v.reshape(v.shape[:-1] + (-1, 32))
    amax = np.abs(blocks).max(-1, keepdims=True)
    byte = np.maximum(np.where(amax > 0, np.frexp(amax)[1] - 1 + 127, 0) - down, 1)
    scale = np.exp2(byte - 127.0)
    codes = (blocks / scale).astype(np.float32).astype(dtype).astype(np.float64)
    return np.moveaxis((codes * scale).reshape(v.shape), -1, axis)


WIDE = False


def mx_kscale(k):
    if not WIDE:
        return np.ones(k)
    levels = np.array([10, -10, 5, -5, 0])
    if k % 512:
        return np.exp2(np.random.permutation(np.resize(levels, k // 32))).repeat(32)
    a = np.empty((k // 512, 16))
    for p in range(k // 512):
        a[p, :8] = np.random.permutation(np.resize(levels, 8))
        for g in range(8):
            far = levels[np.abs(levels - a[p, g]) >= 10]
            a[p, g + 8] = far[np.random.randint(len(far))]
    return np.exp2(a.ravel()).repeat(32)


def f64(x):
    return np.asarray(x).astype(np.float64)


def striped(idx):
    return np.tile(idx.reshape(-1, 16).T, (8, 1)).astype(np.uint16)


def unstriped(offs):
    return offs[:16].T.reshape(-1).astype(np.int64)


K, T, D, S, V, N = 512, 1024, 3, 1536, 512, 256
P = 2 ** 7


def setup_inputs():
    n = np.random.standard_normal
    s = mx_kscale(K)[:, None]
    return {
        "xT": (n((K, T)) * s / np.sqrt(D)).astype(ml_dtypes.bfloat16).astype(np.float32),
        "w": (n((K, N)) / np.sqrt(K) / s).astype(np.float32),
        "gate": np.tile(np.random.uniform(0.5, 1.5, (D, 1, V)), (1, P, 1)).astype(ml_dtypes.bfloat16).astype(np.float32),
        "offs": striped(np.concatenate([np.random.permutation(T)[:V] for _ in range(D)])),
    }


def reference(xT, w, gate, offs):
    idx = unstriped(offs)
    x = sum(f64(gate)[d, :1] * f64(xT)[:, idx[d * V:(d + 1) * V]] for d in range(D))
    return mxq(f64(w), 0, "e4m3").T @ mxq(x, 0, "e4m3")

@@ -1,0 +1,156 @@
+from contextlib import ExitStack
+
+import concourse.mybir as mybir
+from concourse.masks import make_identity
+
+K, T, D, V, N = 512, 1024, 3, 512, 256
+FLOPS = 2 * K * V * N
+BYTES = 4 * (K * T + K * N + D * V + N * V) + 2 * 128 * (D * V // 16)
+
+F32 = mybir.dt.float32
+BF16 = mybir.dt.bfloat16
+U32 = mybir.dt.uint32
+U16 = mybir.dt.uint16
+U8 = mybir.dt.uint8
+FP8X4 = mybir.dt.float8_e4m3fn_x4
+COPY = mybir.ActivationFunctionType.Copy
+MULT = mybir.AluOpType.mult
+ADD = mybir.AluOpType.add
+
+P = 128
+CHUNKS = V // P
+LOADS = (((0, 512), (512, 768), (768, 1024)), ((0, 512), (512, 1024)))
+VECTOR_LAST = 176
+
+
+def tile_picked_bag_lin_none_sub_l_kernel(tc, xT, w, gate, offs, out):
+    nc = tc.nc
+    with ExitStack() as ctx:
+        keep = ctx.enter_context(tc.tile_pool(name="keep", bufs=1))
+        psum = ctx.enter_context(tc.psum_pool(name="psum", bufs=8))
+
+        offsets = keep.tile([P, D * V // 16], U16, name="offsets")
+        x_rows = xT.rearrange("(p j) t -> p j t", j=4)
+        raw = {}
+        for u in range(2):
+            for a, b in LOADS[u]:
+                raw[u, a] = keep.tile([P, 2, b - a], F32, name="raw%d_%d" % (u, a))
+        gate_rows = keep.tile([P, V], F32, name="gate_rows")
+        w_raw = keep.tile([P, 4, N], F32, name="w_raw")
+        ident = keep.tile([P, P], F32, name="ident")
+        warm = keep.tile([P, 8], F32, name="warm")
+
+        nc.gpsimd.memset(gate_rows[:], 0.0)
+        make_identity(nc, ident[:])
+        nc.vector.memset(warm[:], 0.0)
+        nc.scalar.activation(warm[:, 4:8], warm[:, 0:4], COPY, scale=warm[:, 0:1])
+
+        def load_x(u):
+            for a, b in LOADS[u]:
+                nc.sync.dma_start(out=raw[u, a][:], in_=x_rows[:, 2 * u : 2 * u + 2, a:b])
+
+        load_x(0)
+        nc.sync.dma_start(offsets[:], offs)
+        nc.sync.dma_start(out=gate_rows[0:D, :], in_=gate[:, 0, :])
+        load_x(1)
+        nc.sync.dma_start(out=w_raw[:], in_=w.rearrange("(p j) m -> p j m", j=4))
+
+        pairs = [keep.tile([P, T, 2], BF16, name="pairs%d" % u, align_bytes=64) for u in range(2)]
+
+        def cast(copy, u, start, a, b):
+            copy(pairs[u][:, start + a : start + b, :], raw[u, start][:, :, a:b].rearrange("p e t -> p t e"))
+
+        for a, b in LOADS[0][:-1]:
+            cast(nc.vector.tensor_copy, 0, a, 0, b - a)
+        a, b = LOADS[0][-1]
+        cast(nc.vector.tensor_copy, 0, a, 0, VECTOR_LAST)
+        cast(nc.scalar.copy, 0, a, VECTOR_LAST, b - a)
+
+        gate_bank = psum.tile([P, CHUNKS, P], F32, tag="bank", name="gate_bank")
+        for c in range(CHUNKS):
+            nc.tensor.transpose(gate_bank[:, c, :], gate_rows[:, c * P : (c + 1) * P], ident[:])
+        gate_cols = keep.tile([P, CHUNKS, 4], F32, name="gate_cols")
+        nc.scalar.copy(gate_cols[:], gate_bank[:, :, 0:4])
+
+        for a, b in LOADS[1]:
+            cast(nc.scalar.copy, 1, a, 0, b - a)
+
+        turned = {}
+        for d in range(D):
+            for half in range(2):
+                turned[d, half] = psum.tile([P, 2, 2, P], F32, tag="bank", name="turned%d%d" % (d, half))
+
+        def gather_and_turn(u, d):
+            words = keep.tile([P, V], U32, name="words%d%d" % (u, d))
+            window = pairs[u][:].rearrange("p t e -> p (t e)").bitcast(U32)
+            nc.vector.tensor_copy(words[:], window.indirect(offsets[:, d * V // 16 : (d + 1) * V // 16]))
+            for c in range(CHUNKS):
+                nc.tensor.transpose(turned[d, c // 2][:, c % 2, u, :], words[:, c * P : (c + 1) * P].bitcast(F32), ident[:])
+
+        def values(d, c):
+            return turned[d, c // 2][:, c % 2, :, :].rearrange("v u p -> v (u p)").bitcast(BF16)
+
+        one_term = [keep.tile([P, K], F32, name="one_term%d" % c) for c in range(CHUNKS)]
+        two_terms = [keep.tile([P, K], F32, name="two_terms%d" % c) for c in range(CHUNKS)]
+        sums = [keep.tile([P, K], BF16, name="sums%d" % c) for c in range(CHUNKS)]
+        grouped = [keep.tile([P, 4 * P], BF16, name="grouped%d" % c, align_bytes=64) for c in range(CHUNKS)]
+
+        def first_term(c):
+            nc.scalar.activation(one_term[c][:], values(0, c), COPY, scale=gate_cols[:, c, 0:1])
+
+        def second_term(c):
+            nc.vector.scalar_tensor_tensor(two_terms[c][:], values(1, c), gate_cols[:, c, 1:2], one_term[c][:], MULT, ADD)
+
+        def third_term(c):
+            nc.vector.scalar_tensor_tensor(sums[c][:], values(2, c), gate_cols[:, c, 2:3], two_terms[c][:], MULT, ADD)
+            bank = psum.tile([P, 2, P], F32, tag="bank", name="back%d" % c)
+            for u in range(2):
+                nc.tensor.transpose(bank[:, u, :], sums[c][:, 2 * P * u : 2 * P * (u + 1)].bitcast(F32), ident[:])
+            nc.scalar.copy(grouped[c][:].bitcast(F32).rearrange("p (v u) -> p v u", u=2), bank[:].rearrange("p u v -> p v u"))
+
+        w_grouped = keep.tile([P, N, 4], BF16, name="w_grouped", align_bytes=64)
+        w_codes = keep.tile([P, N], U32, name="w_codes", align_bytes=64)
+        w_scales = keep.tile([P, N], U8, name="w_scales", align_bytes=64)
+        out_rows = out.rearrange("(h p) v -> p h v", p=P)
+
+        def multiply(c):
+            codes = keep.tile([P, P], U32, name="codes%d" % c, align_bytes=64)
+            scales = keep.tile([P, P], U8, name="scales%d" % c, align_bytes=64)
+            nc.vector.quantize_mx(out=codes[:].bitcast(FP8X4), scales=scales[:], in_=grouped[c][:])
+            result = keep.tile([P, 2, P], F32, name="result%d" % c)
+            bank = psum.tile([P, 2, P], F32, tag="bank", name="product%d" % c)
+            for h in range(2):
+                rows = slice(h * P, (h + 1) * P)
+                nc.tensor.matmul_mx(
+                    out=bank[:, h, :],
+                    lhsT=w_codes[:, rows].bitcast(FP8X4),
+                    lhsT_scale=w_scales[:, rows],
+                    rhs=codes[:].bitcast(FP8X4),
+                    rhs_scale=scales[:],
+                    start=True,
+                    stop=True,
+                )
+            nc.scalar.copy(result[:], bank[:])
+            nc.sync.dma_start(out=out_rows[:, :, c * P : (c + 1) * P], in_=result[:])
+
+        for d in range(D):
+            gather_and_turn(0, d)
+        nc.scalar.copy(w_grouped[:], w_raw[:].rearrange("p j m -> p m j"))
+        gather_and_turn(1, 0)
+        for c in range(CHUNKS):
+            first_term(c)
+        gather_and_turn(1, 1)
+        gather_and_turn(1, 2)
+        nc.vector.quantize_mx(out=w_codes[:].bitcast(FP8X4), scales=w_scales[:], in_=w_grouped[:].rearrange("p m j -> p (m j)"))
+        second_term(0)
+        second_term(1)
+        third_term(0)
+        second_term(2)
+        third_term(1)
+        multiply(0)
+        second_term(3)
+        third_term(2)
+        multiply(1)
+        third_term(3)
+        multiply(2)
+        multiply(3)

@@ -19,8 +19,9 @@ ADD = mybir.AluOpType.add
 
 P = 128
 CHUNKS = V // P
-LOADS = (((0, 512), (512, 768), (768, 1024)), ((0, 512), (512, 1024)))
-VECTOR_LAST = 176
+PE_SUMMED = (0, 1)
+VECTOR_SUMMED = (2, 3)
+LOW_LOADS = (((0, 512), (512, 768), (768, 1024)), ((0, 512), (512, 1024)))
 
 
 def tile_picked_bag_lin_none_sub_l_kernel(tc, xT, w, gate, offs, out):
@@ -31,10 +32,11 @@ def tile_picked_bag_lin_none_sub_l_kernel(tc, xT, w, gate, offs, out):
 
         offsets = keep.tile([P, D * V // 16], U16, name="offsets")
         x_rows = xT.rearrange("(p j) t -> p j t", j=4)
-        raw = {}
+        pairs = [keep.tile([P, T], F32, name="pairs%d" % u, align_bytes=64) for u in range(2)]
+        low = {}
         for u in range(2):
-            for a, b in LOADS[u]:
-                raw[u, a] = keep.tile([P, 2, b - a], F32, name="raw%d_%d" % (u, a))
+            for a, b in LOW_LOADS[u]:
+                low[u, a] = keep.tile([P, b - a], F32, name="low%d_%d" % (u, a))
         gate_rows = keep.tile([P, V], F32, name="gate_rows")
         w_raw = keep.tile([P, 4, N], F32, name="w_raw")
         ident = keep.tile([P, P], F32, name="ident")
@@ -46,8 +48,9 @@ def tile_picked_bag_lin_none_sub_l_kernel(tc, xT, w, gate, offs, out):
         nc.scalar.activation(warm[:, 4:8], warm[:, 0:4], COPY, scale=warm[:, 0:1])
 
         def load_x(u):
-            for a, b in LOADS[u]:
-                nc.sync.dma_start(out=raw[u, a][:], in_=x_rows[:, 2 * u : 2 * u + 2, a:b])
+            nc.sync.dma_start(out=pairs[u][:], in_=x_rows[:, 2 * u + 1, :])
+            for a, b in LOW_LOADS[u]:
+                nc.sync.dma_start(out=low[u, a][:], in_=x_rows[:, 2 * u, a:b])
 
         load_x(0)
         nc.sync.dma_start(offsets[:], offs)
@@ -55,16 +58,15 @@ def tile_picked_bag_lin_none_sub_l_kernel(tc, xT, w, gate, offs, out):
         load_x(1)
         nc.sync.dma_start(out=w_raw[:], in_=w.rearrange("(p j) m -> p j m", j=4))
 
-        pairs = [keep.tile([P, T, 2], BF16, name="pairs%d" % u, align_bytes=64) for u in range(2)]
+        def gpsimd_cast(dst, src):
+            nc.gpsimd.tensor_scalar(dst, src, 1.0, 0.0, MULT, ADD)
 
-        def cast(copy, u, start, a, b):
-            copy(pairs[u][:, start + a : start + b, :], raw[u, start][:, :, a:b].rearrange("p e t -> p t e"))
+        def fill_low_halves(copy, u):
+            halves = pairs[u][:].bitcast(BF16).rearrange("p (t e) -> p t e", e=2)
+            for a, b in LOW_LOADS[u]:
+                copy(halves[:, a:b, 0], low[u, a][:])
 
-        for a, b in LOADS[0][:-1]:
-            cast(nc.vector.tensor_copy, 0, a, 0, b - a)
-        a, b = LOADS[0][-1]
-        cast(nc.vector.tensor_copy, 0, a, 0, VECTOR_LAST)
-        cast(nc.scalar.copy, 0, a, VECTOR_LAST, b - a)
+        fill_low_halves(nc.vector.tensor_copy, 0)
 
         gate_bank = psum.tile([P, CHUNKS, P], F32, tag="bank", name="gate_bank")
         for c in range(CHUNKS):
@@ -72,31 +74,49 @@ def tile_picked_bag_lin_none_sub_l_kernel(tc, xT, w, gate, offs, out):
         gate_cols = keep.tile([P, CHUNKS, 4], F32, name="gate_cols")
         nc.scalar.copy(gate_cols[:], gate_bank[:, :, 0:4])
 
-        for a, b in LOADS[1]:
-            cast(nc.scalar.copy, 1, a, 0, b - a)
+        fill_low_halves(gpsimd_cast, 1)
 
+        held = {d: psum.tile([P, 2, 2, P], F32, tag="bank", name="held%d" % d) for d in (1, 2)}
+        acc = {c: psum.tile([P, 4, P], F32, tag="bank", name="acc%d" % c) for c in PE_SUMMED}
         turned = {}
-        for d in range(D):
-            for half in range(2):
-                turned[d, half] = psum.tile([P, 2, 2, P], F32, tag="bank", name="turned%d%d" % (d, half))
 
-        def gather_and_turn(u, d):
-            words = keep.tile([P, V], U32, name="words%d%d" % (u, d))
-            window = pairs[u][:].rearrange("p t e -> p (t e)").bitcast(U32)
-            nc.vector.tensor_copy(words[:], window.indirect(offsets[:, d * V // 16 : (d + 1) * V // 16]))
-            for c in range(CHUNKS):
-                nc.tensor.transpose(turned[d, c // 2][:, c % 2, u, :], words[:, c * P : (c + 1) * P].bitcast(F32), ident[:])
+        def gather_and_turn(u, d, chunks):
+            n = len(chunks) * P
+            first = d * V + chunks[0] * P
+            words = keep.tile([P, n], U32, name="words%d%d%d" % (u, d, chunks[0]))
+            nc.vector.tensor_copy(words[:], pairs[u][:].bitcast(U32).indirect(offsets[:, first // 16 : (first + n) // 16]))
+            passing = [c for c in chunks if d == 0 or c in PE_SUMMED]
+            if passing:
+                bank = psum.tile([P, CHUNKS, P], F32, tag="bank", name="turned%d%d%d" % (u, d, chunks[0]))
+            for i, c in enumerate(chunks):
+                turned[u, d, c] = bank[:, i, :] if c in passing else held[d][:, VECTOR_SUMMED.index(c), u, :]
+                nc.tensor.transpose(turned[u, d, c], words[:, i * P : (i + 1) * P].bitcast(F32), ident[:])
 
-        def values(d, c):
-            return turned[d, c // 2][:, c % 2, :, :].rearrange("v u p -> v (u p)").bitcast(BF16)
-
-        one_term = [keep.tile([P, K], F32, name="one_term%d" % c) for c in range(CHUNKS)]
-        two_terms = [keep.tile([P, K], F32, name="two_terms%d" % c) for c in range(CHUNKS)]
-        sums = [keep.tile([P, K], BF16, name="sums%d" % c) for c in range(CHUNKS)]
+        term = {}
+        one_term = {c: keep.tile([P, K], F32, name="one_term%d" % c) for c in VECTOR_SUMMED}
+        two_terms = {c: keep.tile([P, K], F32, name="two_terms%d" % c) for c in VECTOR_SUMMED}
+        sums = {c: keep.tile([P, K], BF16, name="sums%d" % c) for c in VECTOR_SUMMED}
         grouped = [keep.tile([P, 4 * P], BF16, name="grouped%d" % c, align_bytes=64) for c in range(CHUNKS)]
 
-        def first_term(c):
-            nc.scalar.activation(one_term[c][:], values(0, c), COPY, scale=gate_cols[:, c, 0:1])
+        def scale(u, d, chunks):
+            for c in chunks:
+                values = turned[u, d, c].bitcast(BF16)
+                if c in PE_SUMMED:
+                    term[u, d, c] = keep.tile([P, 2, P], F32, name="term%d%d%d" % (u, d, c))
+                    nc.scalar.activation(term[u, d, c][:], values.rearrange("v (p e) -> v e p", e=2), COPY, scale=gate_cols[:, c, d : d + 1])
+                else:
+                    nc.scalar.activation(one_term[c][:, 2 * P * u : 2 * P * (u + 1)], values, COPY, scale=gate_cols[:, c, d : d + 1])
+
+        def sum_back(u, c):
+            for e in range(2):
+                for d in range(D):
+                    nc.tensor.matmul(acc[c][:, 2 * u + e, :], term[u, d, c][:, e, :], ident[:], start=(d == 0), stop=(d == D - 1), is_transpose=True)
+
+        def round_sums(c):
+            nc.scalar.copy(grouped[c][:].rearrange("p (v t) -> p v t", t=4), acc[c][:].rearrange("p t v -> p v t"))
+
+        def values(d, c):
+            return held[d][:, VECTOR_SUMMED.index(c), :, :].rearrange("v u p -> v (u p)").bitcast(BF16)
 
         def second_term(c):
             nc.vector.scalar_tensor_tensor(two_terms[c][:], values(1, c), gate_cols[:, c, 1:2], one_term[c][:], MULT, ADD)
@@ -113,16 +133,16 @@ def tile_picked_bag_lin_none_sub_l_kernel(tc, xT, w, gate, offs, out):
         w_scales = keep.tile([P, N], U8, name="w_scales", align_bytes=64)
         out_rows = out.rearrange("(h p) v -> p h v", p=P)
 
-        def multiply(c):
+        def multiply(c, copies):
             codes = keep.tile([P, P], U32, name="codes%d" % c, align_bytes=64)
             scales = keep.tile([P, P], U8, name="scales%d" % c, align_bytes=64)
             nc.vector.quantize_mx(out=codes[:].bitcast(FP8X4), scales=scales[:], in_=grouped[c][:])
             result = keep.tile([P, 2, P], F32, name="result%d" % c)
-            bank = psum.tile([P, 2, P], F32, tag="bank", name="product%d" % c)
+            banks = [psum.tile([P, 2, P], F32, tag="bank", name="product%d%d" % (c, i)) for i in range(len(copies))]
             for h in range(2):
                 rows = slice(h * P, (h + 1) * P)
                 nc.tensor.matmul_mx(
-                    out=bank[:, h, :],
+                    out=banks[h % len(copies)][:, h, :],
                     lhsT=w_codes[:, rows].bitcast(FP8X4),
                     lhsT_scale=w_scales[:, rows],
                     rhs=codes[:].bitcast(FP8X4),
@@ -130,27 +150,40 @@ def tile_picked_bag_lin_none_sub_l_kernel(tc, xT, w, gate, offs, out):
                     start=True,
                     stop=True,
                 )
-            nc.scalar.copy(result[:], bank[:])
+            if len(copies) == 1:
+                copies[0](result[:], banks[0][:])
+            else:
+                for h in range(2):
+                    copies[h](result[:, h, :], banks[h][:, h, :])
             nc.sync.dma_start(out=out_rows[:, :, c * P : (c + 1) * P], in_=result[:])
 
+        every = PE_SUMMED + VECTOR_SUMMED
+        gather_and_turn(0, 0, every)
+        scale(0, 0, PE_SUMMED)
+        gather_and_turn(0, 1, every)
+        scale(0, 1, PE_SUMMED)
+        scale(0, 0, VECTOR_SUMMED)
+        gather_and_turn(0, 2, every)
+        scale(0, 2, PE_SUMMED)
+        gpsimd_cast(w_grouped[:], w_raw[:].rearrange("p j m -> p m j"))
         for d in range(D):
-            gather_and_turn(0, d)
-        nc.scalar.copy(w_grouped[:], w_raw[:].rearrange("p j m -> p m j"))
-        gather_and_turn(1, 0)
-        for c in range(CHUNKS):
-            first_term(c)
-        gather_and_turn(1, 1)
-        gather_and_turn(1, 2)
+            gather_and_turn(1, d, PE_SUMMED)
+            scale(1, d, PE_SUMMED)
+            if d < 2:
+                sum_back(0, PE_SUMMED[d])
+        for d in range(D):
+            gather_and_turn(1, d, VECTOR_SUMMED)
+            if d == 0:
+                scale(1, d, VECTOR_SUMMED)
+        for c in PE_SUMMED:
+            sum_back(1, c)
+            round_sums(c)
         nc.vector.quantize_mx(out=w_codes[:].bitcast(FP8X4), scales=w_scales[:], in_=w_grouped[:].rearrange("p m j -> p (m j)"))
-        second_term(0)
-        second_term(1)
-        third_term(0)
         second_term(2)
-        third_term(1)
-        multiply(0)
         second_term(3)
         third_term(2)
-        multiply(1)
+        multiply(0, [nc.scalar.copy])
         third_term(3)
-        multiply(2)
-        multiply(3)
+        multiply(1, [nc.scalar.copy])
+        multiply(2, [nc.vector.tensor_copy])
+        multiply(3, [nc.scalar.copy, nc.vector.tensor_copy])

@@ -18,27 +18,42 @@ MULT = mybir.AluOpType.mult
 ADD = mybir.AluOpType.add
 
 P = 128
+PACK = 4
 CHUNKS = V // P
-PE_SUMMED = (0, 1)
+BANKS = 8
+TENSOR_SUMMED = (0, 1)
 VECTOR_SUMMED = (2, 3)
-LOW_LOADS = (((0, 512), (512, 768), (768, 1024)), ((0, 512), (512, 1024)))
+EVEN_LOADS = ((0, 512), (512, 768), (768, 1024))
 
 
 def tile_picked_bag_lin_none_sub_l_kernel(tc, xT, w, gate, offs, out):
     nc = tc.nc
     with ExitStack() as ctx:
         keep = ctx.enter_context(tc.tile_pool(name="keep", bufs=1))
-        psum = ctx.enter_context(tc.psum_pool(name="psum", bufs=8))
+        psum = ctx.enter_context(tc.psum_pool(name="psum", bufs=1))
+
+        free_banks = list(range(BANKS))
+        bank_number = {}
+
+        def take_bank(name, shape):
+            bank_number[name] = free_banks.pop(0)
+            return psum.tile(shape, F32, tag="bank%d" % bank_number[name], name=name)
+
+        def give_bank(name):
+            free_banks.append(bank_number[name])
+
+        def gpsimd_cast(dst, src):
+            nc.gpsimd.tensor_scalar(dst, src, 1.0, 0.0, MULT, ADD)
 
         offsets = keep.tile([P, D * V // 16], U16, name="offsets")
-        x_rows = xT.rearrange("(p j) t -> p j t", j=4)
+        x_rows = xT.rearrange("(p t) i -> p t i", t=PACK)
         pairs = [keep.tile([P, T], F32, name="pairs%d" % u, align_bytes=64) for u in range(2)]
-        low = {}
+        even = {}
         for u in range(2):
-            for a, b in LOW_LOADS[u]:
-                low[u, a] = keep.tile([P, b - a], F32, name="low%d_%d" % (u, a))
+            for a, b in EVEN_LOADS:
+                even[u, a] = keep.tile([P, b - a], F32, name="even%d_%d" % (u, a))
         gate_rows = keep.tile([P, V], F32, name="gate_rows")
-        w_raw = keep.tile([P, 4, N], F32, name="w_raw")
+        w_raw = keep.tile([P, PACK, N], F32, name="w_raw")
         ident = keep.tile([P, P], F32, name="ident")
         warm = keep.tile([P, 8], F32, name="warm")
 
@@ -47,143 +62,142 @@ def tile_picked_bag_lin_none_sub_l_kernel(tc, xT, w, gate, offs, out):
         nc.vector.memset(warm[:], 0.0)
         nc.scalar.activation(warm[:, 4:8], warm[:, 0:4], COPY, scale=warm[:, 0:1])
 
-        def load_x(u):
+        def load_pair(u):
             nc.sync.dma_start(out=pairs[u][:], in_=x_rows[:, 2 * u + 1, :])
-            for a, b in LOW_LOADS[u]:
-                nc.sync.dma_start(out=low[u, a][:], in_=x_rows[:, 2 * u, a:b])
+            for a, b in EVEN_LOADS:
+                nc.sync.dma_start(out=even[u, a][:], in_=x_rows[:, 2 * u, a:b])
 
-        load_x(0)
+        load_pair(0)
         nc.sync.dma_start(offsets[:], offs)
         nc.sync.dma_start(out=gate_rows[0:D, :], in_=gate[:, 0, :])
-        load_x(1)
-        nc.sync.dma_start(out=w_raw[:], in_=w.rearrange("(p j) m -> p j m", j=4))
+        load_pair(1)
+        nc.sync.dma_start(out=w_raw[:], in_=w.rearrange("(p t) m -> p t m", t=PACK))
 
-        def gpsimd_cast(dst, src):
-            nc.gpsimd.tensor_scalar(dst, src, 1.0, 0.0, MULT, ADD)
+        def fill_low_halves(u, casts):
+            halves = pairs[u][:].bitcast(BF16).rearrange("p (i e) -> p i e", e=2)
+            for (a, b), cast in zip(EVEN_LOADS, casts):
+                cast(halves[:, a:b, 0], even[u, a][:])
 
-        def fill_low_halves(copy, u):
-            halves = pairs[u][:].bitcast(BF16).rearrange("p (t e) -> p t e", e=2)
-            for a, b in LOW_LOADS[u]:
-                copy(halves[:, a:b, 0], low[u, a][:])
+        fill_low_halves(0, [nc.vector.tensor_copy] * len(EVEN_LOADS))
 
-        fill_low_halves(nc.vector.tensor_copy, 0)
-
-        gate_bank = psum.tile([P, CHUNKS, P], F32, tag="bank", name="gate_bank")
+        gate_bank = take_bank("gate_bank", [P, CHUNKS, P])
         for c in range(CHUNKS):
             nc.tensor.transpose(gate_bank[:, c, :], gate_rows[:, c * P : (c + 1) * P], ident[:])
-        gate_cols = keep.tile([P, CHUNKS, 4], F32, name="gate_cols")
-        nc.scalar.copy(gate_cols[:], gate_bank[:, :, 0:4])
+        gate_cols = keep.tile([P, CHUNKS, D + 1], F32, name="gate_cols")
+        nc.scalar.copy(gate_cols[:], gate_bank[:, :, 0 : D + 1])
+        give_bank("gate_bank")
 
-        fill_low_halves(gpsimd_cast, 1)
+        fill_low_halves(1, [gpsimd_cast, nc.scalar.copy, gpsimd_cast])
 
-        held = {d: psum.tile([P, 2, 2, P], F32, tag="bank", name="held%d" % d) for d in (1, 2)}
-        acc = {c: psum.tile([P, 4, P], F32, tag="bank", name="acc%d" % c) for c in PE_SUMMED}
-        turned = {}
+        held = {d: take_bank("held%d" % d, [P, 2, 2, P]) for d in (1, 2)}
+        term = {}
+        acc = {}
+        one_term = {c: keep.tile([P, K], F32, name="one_term%d" % c) for c in VECTOR_SUMMED}
+        two_terms = {c: keep.tile([P, K], F32, name="two_terms%d" % c) for c in VECTOR_SUMMED}
+        sums = {c: keep.tile([P, K], BF16, name="sums%d" % c) for c in VECTOR_SUMMED}
+        grouped = [keep.tile([P, PACK * P], BF16, name="grouped%d" % c, align_bytes=64) for c in range(CHUNKS)]
 
-        def gather_and_turn(u, d, chunks):
+        def gather(u, d, chunks):
             n = len(chunks) * P
             first = d * V + chunks[0] * P
             words = keep.tile([P, n], U32, name="words%d%d%d" % (u, d, chunks[0]))
             nc.vector.tensor_copy(words[:], pairs[u][:].bitcast(U32).indirect(offsets[:, first // 16 : (first + n) // 16]))
-            passing = [c for c in chunks if d == 0 or c in PE_SUMMED]
-            if passing:
-                bank = psum.tile([P, CHUNKS, P], F32, tag="bank", name="turned%d%d%d" % (u, d, chunks[0]))
+            if chunks == VECTOR_SUMMED and d > 0:
+                for i in range(len(chunks)):
+                    nc.tensor.transpose(held[d][:, i, u, :], words[:, i * P : (i + 1) * P].bitcast(F32), ident[:])
+                return
+            name = "turned%d%d%d" % (u, d, chunks[0])
+            bank = take_bank(name, [P, len(chunks), P])
+            for i in range(len(chunks)):
+                nc.tensor.transpose(bank[:, i, :], words[:, i * P : (i + 1) * P].bitcast(F32), ident[:])
             for i, c in enumerate(chunks):
-                turned[u, d, c] = bank[:, i, :] if c in passing else held[d][:, VECTOR_SUMMED.index(c), u, :]
-                nc.tensor.transpose(turned[u, d, c], words[:, i * P : (i + 1) * P].bitcast(F32), ident[:])
-
-        term = {}
-        one_term = {c: keep.tile([P, K], F32, name="one_term%d" % c) for c in VECTOR_SUMMED}
-        two_terms = {c: keep.tile([P, K], F32, name="two_terms%d" % c) for c in VECTOR_SUMMED}
-        sums = {c: keep.tile([P, K], BF16, name="sums%d" % c) for c in VECTOR_SUMMED}
-        grouped = [keep.tile([P, 4 * P], BF16, name="grouped%d" % c, align_bytes=64) for c in range(CHUNKS)]
-
-        def scale(u, d, chunks):
-            for c in chunks:
-                values = turned[u, d, c].bitcast(BF16)
-                if c in PE_SUMMED:
-                    term[u, d, c] = keep.tile([P, 2, P], F32, name="term%d%d%d" % (u, d, c))
-                    nc.scalar.activation(term[u, d, c][:], values.rearrange("v (p e) -> v e p", e=2), COPY, scale=gate_cols[:, c, d : d + 1])
+                values = bank[:, i, :].bitcast(BF16)
+                weight = gate_cols[:, c, d : d + 1]
+                if chunks == VECTOR_SUMMED:
+                    nc.scalar.activation(one_term[c][:, 2 * P * u : 2 * P * (u + 1)], values, COPY, scale=weight)
                 else:
-                    nc.scalar.activation(one_term[c][:, 2 * P * u : 2 * P * (u + 1)], values, COPY, scale=gate_cols[:, c, d : d + 1])
+                    term[u, d, c] = keep.tile([P, 2, P], F32, name="term%d%d%d" % (u, d, c))
+                    nc.scalar.activation(term[u, d, c][:], values.rearrange("v (p e) -> v e p", e=2), COPY, scale=weight)
+            give_bank(name)
 
         def sum_back(u, c):
+            if u == 0:
+                acc[c] = take_bank("acc%d" % c, [P, PACK, P])
             for e in range(2):
                 for d in range(D):
                     nc.tensor.matmul(acc[c][:, 2 * u + e, :], term[u, d, c][:, e, :], ident[:], start=(d == 0), stop=(d == D - 1), is_transpose=True)
 
         def round_sums(c):
-            nc.scalar.copy(grouped[c][:].rearrange("p (v t) -> p v t", t=4), acc[c][:].rearrange("p t v -> p v t"))
+            nc.scalar.copy(grouped[c][:].rearrange("p (v t) -> p v t", t=PACK), acc[c][:].rearrange("p t v -> p v t"))
+            give_bank("acc%d" % c)
 
-        def values(d, c):
-            return held[d][:, VECTOR_SUMMED.index(c), :, :].rearrange("v u p -> v (u p)").bitcast(BF16)
+        def add_term(d, src, dst):
+            for i, c in enumerate(VECTOR_SUMMED):
+                values = held[d][:, i, :, :].rearrange("v u p -> v (u p)").bitcast(BF16)
+                nc.vector.scalar_tensor_tensor(dst[c][:], values, gate_cols[:, c, d : d + 1], src[c][:], MULT, ADD)
+            give_bank("held%d" % d)
 
-        def second_term(c):
-            nc.vector.scalar_tensor_tensor(two_terms[c][:], values(1, c), gate_cols[:, c, 1:2], one_term[c][:], MULT, ADD)
-
-        def third_term(c):
-            nc.vector.scalar_tensor_tensor(sums[c][:], values(2, c), gate_cols[:, c, 2:3], two_terms[c][:], MULT, ADD)
-            bank = psum.tile([P, 2, P], F32, tag="bank", name="back%d" % c)
+        def turn_back(c):
+            bank = take_bank("back%d" % c, [P, 2, P])
             for u in range(2):
                 nc.tensor.transpose(bank[:, u, :], sums[c][:, 2 * P * u : 2 * P * (u + 1)].bitcast(F32), ident[:])
             nc.scalar.copy(grouped[c][:].bitcast(F32).rearrange("p (v u) -> p v u", u=2), bank[:].rearrange("p u v -> p v u"))
+            give_bank("back%d" % c)
 
-        w_grouped = keep.tile([P, N, 4], BF16, name="w_grouped", align_bytes=64)
+        w_grouped = keep.tile([P, N, PACK], BF16, name="w_grouped", align_bytes=64)
         w_codes = keep.tile([P, N], U32, name="w_codes", align_bytes=64)
         w_scales = keep.tile([P, N], U8, name="w_scales", align_bytes=64)
+        x_codes = [keep.tile([P, P], U32, name="x_codes%d" % c, align_bytes=64) for c in range(CHUNKS)]
+        x_scales = [keep.tile([P, P], U8, name="x_scales%d" % c, align_bytes=64) for c in range(CHUNKS)]
         out_rows = out.rearrange("(h p) v -> p h v", p=P)
 
-        def multiply(c, copies):
-            codes = keep.tile([P, P], U32, name="codes%d" % c, align_bytes=64)
-            scales = keep.tile([P, P], U8, name="scales%d" % c, align_bytes=64)
-            nc.vector.quantize_mx(out=codes[:].bitcast(FP8X4), scales=scales[:], in_=grouped[c][:])
+        def multiply(c, split):
             result = keep.tile([P, 2, P], F32, name="result%d" % c)
-            banks = [psum.tile([P, 2, P], F32, tag="bank", name="product%d%d" % (c, i)) for i in range(len(copies))]
+            names = ["product%d%d" % (c, i) for i in range(2 if split else 1)]
+            banks = [take_bank(name, [P, 2, P]) for name in names]
             for h in range(2):
                 rows = slice(h * P, (h + 1) * P)
                 nc.tensor.matmul_mx(
-                    out=banks[h % len(copies)][:, h, :],
+                    out=banks[h if split else 0][:, h, :],
                     lhsT=w_codes[:, rows].bitcast(FP8X4),
                     lhsT_scale=w_scales[:, rows],
-                    rhs=codes[:].bitcast(FP8X4),
-                    rhs_scale=scales[:],
+                    rhs=x_codes[c][:].bitcast(FP8X4),
+                    rhs_scale=x_scales[c][:],
                     start=True,
                     stop=True,
                 )
-            if len(copies) == 1:
-                copies[0](result[:], banks[0][:])
+            if split:
+                nc.scalar.copy(result[:, 0, :], banks[0][:, 0, :])
+                nc.vector.tensor_copy(result[:, 1, :], banks[1][:, 1, :])
             else:
-                for h in range(2):
-                    copies[h](result[:, h, :], banks[h][:, h, :])
+                nc.scalar.copy(result[:], banks[0][:])
+            for name in names:
+                give_bank(name)
             nc.sync.dma_start(out=out_rows[:, :, c * P : (c + 1) * P], in_=result[:])
 
-        every = PE_SUMMED + VECTOR_SUMMED
-        gather_and_turn(0, 0, every)
-        scale(0, 0, PE_SUMMED)
-        gather_and_turn(0, 1, every)
-        scale(0, 1, PE_SUMMED)
-        scale(0, 0, VECTOR_SUMMED)
-        gather_and_turn(0, 2, every)
-        scale(0, 2, PE_SUMMED)
-        gpsimd_cast(w_grouped[:], w_raw[:].rearrange("p j m -> p m j"))
+        for chunks in (TENSOR_SUMMED, VECTOR_SUMMED):
+            for d in range(D):
+                gather(0, d, chunks)
+        gpsimd_cast(w_grouped[:], w_raw[:].rearrange("p t m -> p m t"))
+
+        gather(1, 0, VECTOR_SUMMED)
+        gather(1, 1, VECTOR_SUMMED)
+        for c in TENSOR_SUMMED:
+            sum_back(0, c)
         for d in range(D):
-            gather_and_turn(1, d, PE_SUMMED)
-            scale(1, d, PE_SUMMED)
-            if d < 2:
-                sum_back(0, PE_SUMMED[d])
-        for d in range(D):
-            gather_and_turn(1, d, VECTOR_SUMMED)
-            if d == 0:
-                scale(1, d, VECTOR_SUMMED)
-        for c in PE_SUMMED:
+            gather(1, d, TENSOR_SUMMED)
+        gather(1, 2, VECTOR_SUMMED)
+        for c in TENSOR_SUMMED:
             sum_back(1, c)
+
+        add_term(1, one_term, two_terms)
+        add_term(2, two_terms, sums)
+        nc.vector.quantize_mx(out=w_codes[:].bitcast(FP8X4), scales=w_scales[:], in_=w_grouped[:].rearrange("p m t -> p (m t)"))
+        for c in TENSOR_SUMMED:
             round_sums(c)
-        nc.vector.quantize_mx(out=w_codes[:].bitcast(FP8X4), scales=w_scales[:], in_=w_grouped[:].rearrange("p m j -> p (m j)"))
-        second_term(2)
-        second_term(3)
-        third_term(2)
-        multiply(0, [nc.scalar.copy])
-        third_term(3)
-        multiply(1, [nc.scalar.copy])
-        multiply(2, [nc.vector.tensor_copy])
-        multiply(3, [nc.scalar.copy, nc.vector.tensor_copy])
+        for c in VECTOR_SUMMED:
+            turn_back(c)
+        for c in range(CHUNKS):
+            nc.vector.quantize_mx(out=x_codes[c][:].bitcast(FP8X4), scales=x_scales[c][:], in_=grouped[c][:])
+        for c in range(CHUNKS):
+            multiply(c, split=c > 0)

@@ -21,9 +21,10 @@ P = 128
 PACK = 4
 CHUNKS = V // P
 BANKS = 8
-TENSOR_SUMMED = (0, 1)
-VECTOR_SUMMED = (2, 3)
-EVEN_LOADS = ((0, 512), (512, 768), (768, 1024))
+TENSOR_CHUNK = 0
+MIXED_CHUNK = 1
+VECTOR_CHUNKS = (2, 3)
+EVEN_LOADS = (((0, 640), (640, 1024)), ((0, 384), (384, 768), (768, 1024)))
 
 
 def tile_picked_bag_lin_none_sub_l_kernel(tc, xT, w, gate, offs, out):
@@ -50,7 +51,7 @@ def tile_picked_bag_lin_none_sub_l_kernel(tc, xT, w, gate, offs, out):
         pairs = [keep.tile([P, T], F32, name="pairs%d" % u, align_bytes=64) for u in range(2)]
         even = {}
         for u in range(2):
-            for a, b in EVEN_LOADS:
+            for a, b in EVEN_LOADS[u]:
                 even[u, a] = keep.tile([P, b - a], F32, name="even%d_%d" % (u, a))
         gate_rows = keep.tile([P, V], F32, name="gate_rows")
         w_raw = keep.tile([P, PACK, N], F32, name="w_raw")
@@ -64,7 +65,7 @@ def tile_picked_bag_lin_none_sub_l_kernel(tc, xT, w, gate, offs, out):
 
         def load_pair(u):
             nc.sync.dma_start(out=pairs[u][:], in_=x_rows[:, 2 * u + 1, :])
-            for a, b in EVEN_LOADS:
+            for a, b in EVEN_LOADS[u]:
                 nc.sync.dma_start(out=even[u, a][:], in_=x_rows[:, 2 * u, a:b])
 
         load_pair(0)
@@ -73,12 +74,12 @@ def tile_picked_bag_lin_none_sub_l_kernel(tc, xT, w, gate, offs, out):
         load_pair(1)
         nc.sync.dma_start(out=w_raw[:], in_=w.rearrange("(p t) m -> p t m", t=PACK))
 
-        def fill_low_halves(u, casts):
+        def fill_low_halves(u, cast):
             halves = pairs[u][:].bitcast(BF16).rearrange("p (i e) -> p i e", e=2)
-            for (a, b), cast in zip(EVEN_LOADS, casts):
+            for a, b in EVEN_LOADS[u]:
                 cast(halves[:, a:b, 0], even[u, a][:])
 
-        fill_low_halves(0, [nc.vector.tensor_copy] * len(EVEN_LOADS))
+        fill_low_halves(0, nc.vector.tensor_copy)
 
         gate_bank = take_bank("gate_bank", [P, CHUNKS, P])
         for c in range(CHUNKS):
@@ -87,117 +88,150 @@ def tile_picked_bag_lin_none_sub_l_kernel(tc, xT, w, gate, offs, out):
         nc.scalar.copy(gate_cols[:], gate_bank[:, :, 0 : D + 1])
         give_bank("gate_bank")
 
-        fill_low_halves(1, [gpsimd_cast, nc.scalar.copy, gpsimd_cast])
+        fill_low_halves(1, gpsimd_cast)
 
         held = {d: take_bank("held%d" % d, [P, 2, 2, P]) for d in (1, 2)}
+        turned = {}
+        turned_in = {}
+        readers_left = {}
         term = {}
-        acc = {}
-        one_term = {c: keep.tile([P, K], F32, name="one_term%d" % c) for c in VECTOR_SUMMED}
-        two_terms = {c: keep.tile([P, K], F32, name="two_terms%d" % c) for c in VECTOR_SUMMED}
-        sums = {c: keep.tile([P, K], BF16, name="sums%d" % c) for c in VECTOR_SUMMED}
+        one_term = {c: keep.tile([P, K], F32, name="one_term%d" % c) for c in VECTOR_CHUNKS}
+        two_terms = {c: keep.tile([P, K], F32, name="two_terms%d" % c) for c in VECTOR_CHUNKS}
+        sums = {c: keep.tile([P, K], BF16, name="sums%d" % c) for c in (MIXED_CHUNK,) + VECTOR_CHUNKS}
         grouped = [keep.tile([P, PACK * P], BF16, name="grouped%d" % c, align_bytes=64) for c in range(CHUNKS)]
+
+        def pair_columns(u):
+            return slice(2 * P * u, 2 * P * (u + 1))
+
+        def was_read(u, d, c):
+            readers_left[turned_in[u, d, c]] -= 1
+            if readers_left[turned_in[u, d, c]] == 0:
+                give_bank(turned_in[u, d, c])
+
+        def scale(u, d, c):
+            values = turned[u, d, c].bitcast(BF16)
+            if c in VECTOR_CHUNKS:
+                dst = one_term[c][:, pair_columns(u)]
+            elif c == MIXED_CHUNK:
+                term[u, d, c] = keep.tile([P, 2 * P], F32, name="term%d%d%d" % (u, d, c))
+                dst = term[u, d, c][:]
+            else:
+                term[u, d, c] = keep.tile([P, 2, P], F32, name="term%d%d%d" % (u, d, c))
+                dst = term[u, d, c][:]
+                values = values.rearrange("v (p e) -> v e p", e=2)
+            nc.scalar.activation(dst, values, COPY, scale=gate_cols[:, c, d : d + 1])
+            was_read(u, d, c)
 
         def gather(u, d, chunks):
             n = len(chunks) * P
             first = d * V + chunks[0] * P
             words = keep.tile([P, n], U32, name="words%d%d%d" % (u, d, chunks[0]))
             nc.vector.tensor_copy(words[:], pairs[u][:].bitcast(U32).indirect(offsets[:, first // 16 : (first + n) // 16]))
-            if chunks == VECTOR_SUMMED and d > 0:
-                for i in range(len(chunks)):
-                    nc.tensor.transpose(held[d][:, i, u, :], words[:, i * P : (i + 1) * P].bitcast(F32), ident[:])
-                return
-            name = "turned%d%d%d" % (u, d, chunks[0])
-            bank = take_bank(name, [P, len(chunks), P])
-            for i in range(len(chunks)):
-                nc.tensor.transpose(bank[:, i, :], words[:, i * P : (i + 1) * P].bitcast(F32), ident[:])
+            passing = [c for c in chunks if d == 0 or c not in VECTOR_CHUNKS]
+            if passing:
+                name = "turned%d%d%d" % (u, d, chunks[0])
+                bank = take_bank(name, [P, CHUNKS, P])
+                readers_left[name] = len(passing)
             for i, c in enumerate(chunks):
-                values = bank[:, i, :].bitcast(BF16)
-                weight = gate_cols[:, c, d : d + 1]
-                if chunks == VECTOR_SUMMED:
-                    nc.scalar.activation(one_term[c][:, 2 * P * u : 2 * P * (u + 1)], values, COPY, scale=weight)
+                if c in passing:
+                    turned[u, d, c] = bank[:, i, :]
+                    turned_in[u, d, c] = name
+                    dst = turned[u, d, c]
                 else:
-                    term[u, d, c] = keep.tile([P, 2, P], F32, name="term%d%d%d" % (u, d, c))
-                    nc.scalar.activation(term[u, d, c][:], values.rearrange("v (p e) -> v e p", e=2), COPY, scale=weight)
-            give_bank(name)
+                    dst = held[d][:, VECTOR_CHUNKS.index(c), u, :]
+                nc.tensor.transpose(dst, words[:, i * P : (i + 1) * P].bitcast(F32), ident[:])
+            for c in passing:
+                if d == 0 or c == TENSOR_CHUNK or u == 0:
+                    scale(u, d, c)
 
-        def sum_back(u, c):
-            if u == 0:
-                acc[c] = take_bank("acc%d" % c, [P, PACK, P])
+        def sum_back(acc, u):
             for e in range(2):
                 for d in range(D):
-                    nc.tensor.matmul(acc[c][:, 2 * u + e, :], term[u, d, c][:, e, :], ident[:], start=(d == 0), stop=(d == D - 1), is_transpose=True)
+                    nc.tensor.matmul(
+                        acc[:, 2 * u + e, :], term[u, d, TENSOR_CHUNK][:, e, :], ident[:], start=(d == 0), stop=(d == D - 1), is_transpose=True
+                    )
 
-        def round_sums(c):
-            nc.scalar.copy(grouped[c][:].rearrange("p (v t) -> p v t", t=PACK), acc[c][:].rearrange("p t v -> p v t"))
-            give_bank("acc%d" % c)
+        def add_held(d, c):
+            src, dst = (one_term, two_terms) if d == 1 else (two_terms, sums)
+            values = held[d][:, VECTOR_CHUNKS.index(c), :, :].rearrange("v u p -> v (u p)").bitcast(BF16)
+            nc.vector.scalar_tensor_tensor(dst[c][:], values, gate_cols[:, c, d : d + 1], src[c][:], MULT, ADD)
+            if c == VECTOR_CHUNKS[-1]:
+                give_bank("held%d" % d)
 
-        def add_term(d, src, dst):
-            for i, c in enumerate(VECTOR_SUMMED):
-                values = held[d][:, i, :, :].rearrange("v u p -> v (u p)").bitcast(BF16)
-                nc.vector.scalar_tensor_tensor(dst[c][:], values, gate_cols[:, c, d : d + 1], src[c][:], MULT, ADD)
-            give_bank("held%d" % d)
+        def add_mixed(d, src, dst):
+            values = turned[1, d, MIXED_CHUNK].bitcast(BF16)
+            nc.vector.scalar_tensor_tensor(dst, values, gate_cols[:, MIXED_CHUNK, d : d + 1], src, MULT, ADD)
+            was_read(1, d, MIXED_CHUNK)
 
         def turn_back(c):
             bank = take_bank("back%d" % c, [P, 2, P])
-            for u in range(2):
-                nc.tensor.transpose(bank[:, u, :], sums[c][:, 2 * P * u : 2 * P * (u + 1)].bitcast(F32), ident[:])
+            for u in (1, 0):
+                nc.tensor.transpose(bank[:, u, :], sums[c][:, pair_columns(u)].bitcast(F32), ident[:])
             nc.scalar.copy(grouped[c][:].bitcast(F32).rearrange("p (v u) -> p v u", u=2), bank[:].rearrange("p u v -> p v u"))
             give_bank("back%d" % c)
 
         w_grouped = keep.tile([P, N, PACK], BF16, name="w_grouped", align_bytes=64)
         w_codes = keep.tile([P, N], U32, name="w_codes", align_bytes=64)
         w_scales = keep.tile([P, N], U8, name="w_scales", align_bytes=64)
-        x_codes = [keep.tile([P, P], U32, name="x_codes%d" % c, align_bytes=64) for c in range(CHUNKS)]
-        x_scales = [keep.tile([P, P], U8, name="x_scales%d" % c, align_bytes=64) for c in range(CHUNKS)]
+        x_codes = keep.tile([P, V], U32, name="x_codes", align_bytes=64)
+        x_scales = keep.tile([P, V], U8, name="x_scales", align_bytes=64)
         out_rows = out.rearrange("(h p) v -> p h v", p=P)
 
-        def multiply(c, split):
+        def multiply(c, copies):
+            bags = slice(c * P, (c + 1) * P)
             result = keep.tile([P, 2, P], F32, name="result%d" % c)
-            names = ["product%d%d" % (c, i) for i in range(2 if split else 1)]
+            names = ["product%d%d" % (c, i) for i in range(len(copies))]
             banks = [take_bank(name, [P, 2, P]) for name in names]
             for h in range(2):
                 rows = slice(h * P, (h + 1) * P)
                 nc.tensor.matmul_mx(
-                    out=banks[h if split else 0][:, h, :],
+                    out=banks[h % len(copies)][:, h, :],
                     lhsT=w_codes[:, rows].bitcast(FP8X4),
                     lhsT_scale=w_scales[:, rows],
-                    rhs=x_codes[c][:].bitcast(FP8X4),
-                    rhs_scale=x_scales[c][:],
+                    rhs=x_codes[:, bags].bitcast(FP8X4),
+                    rhs_scale=x_scales[:, bags],
                     start=True,
                     stop=True,
                 )
-            if split:
-                nc.scalar.copy(result[:, 0, :], banks[0][:, 0, :])
-                nc.vector.tensor_copy(result[:, 1, :], banks[1][:, 1, :])
+            if len(copies) == 1:
+                copies[0](result[:], banks[0][:])
             else:
-                nc.scalar.copy(result[:], banks[0][:])
+                for h in range(2):
+                    copies[h](result[:, h, :], banks[h][:, h, :])
             for name in names:
                 give_bank(name)
-            nc.sync.dma_start(out=out_rows[:, :, c * P : (c + 1) * P], in_=result[:])
+            nc.sync.dma_start(out=out_rows[:, :, bags], in_=result[:])
 
-        for chunks in (TENSOR_SUMMED, VECTOR_SUMMED):
-            for d in range(D):
-                gather(0, d, chunks)
-        gpsimd_cast(w_grouped[:], w_raw[:].rearrange("p t m -> p m t"))
-
-        gather(1, 0, VECTOR_SUMMED)
-        gather(1, 1, VECTOR_SUMMED)
-        for c in TENSOR_SUMMED:
-            sum_back(0, c)
         for d in range(D):
-            gather(1, d, TENSOR_SUMMED)
-        gather(1, 2, VECTOR_SUMMED)
-        for c in TENSOR_SUMMED:
-            sum_back(1, c)
+            gather(0, d, tuple(range(CHUNKS)))
+        mixed_two = [keep.tile([P, 2 * P], F32, name="mixed_two%d" % u) for u in range(2)]
+        nc.gpsimd.tensor_tensor(mixed_two[0][:], term[0, 0, MIXED_CHUNK][:], term[0, 1, MIXED_CHUNK][:], ADD)
+        gpsimd_cast(w_grouped[:], w_raw[:].rearrange("p t m -> p m t"))
+        nc.gpsimd.tensor_tensor(sums[MIXED_CHUNK][:, pair_columns(0)], mixed_two[0][:], term[0, 2, MIXED_CHUNK][:], ADD)
+        acc = take_bank("acc", [P, PACK, P])
+        sum_back(acc, 0)
 
-        add_term(1, one_term, two_terms)
-        add_term(2, two_terms, sums)
+        for d in range(D):
+            gather(1, d, (TENSOR_CHUNK, MIXED_CHUNK))
+            gather(1, d, VECTOR_CHUNKS)
+        sum_back(acc, 1)
+
+        add_held(1, VECTOR_CHUNKS[0])
+        add_mixed(1, term[1, 0, MIXED_CHUNK][:], mixed_two[1][:])
+        add_held(1, VECTOR_CHUNKS[1])
+        add_mixed(2, mixed_two[1][:], sums[MIXED_CHUNK][:, pair_columns(1)])
+        for c in VECTOR_CHUNKS:
+            add_held(2, c)
+
         nc.vector.quantize_mx(out=w_codes[:].bitcast(FP8X4), scales=w_scales[:], in_=w_grouped[:].rearrange("p m t -> p (m t)"))
-        for c in TENSOR_SUMMED:
-            round_sums(c)
-        for c in VECTOR_SUMMED:
+        nc.scalar.copy(grouped[TENSOR_CHUNK][:].rearrange("p (v t) -> p v t", t=PACK), acc[:].rearrange("p t v -> p v t"))
+        give_bank("acc")
+        for c in (MIXED_CHUNK,) + VECTOR_CHUNKS:
             turn_back(c)
         for c in range(CHUNKS):
-            nc.vector.quantize_mx(out=x_codes[c][:].bitcast(FP8X4), scales=x_scales[c][:], in_=grouped[c][:])
-        for c in range(CHUNKS):
-            multiply(c, split=c > 0)
+            bags = slice(c * P, (c + 1) * P)
+            nc.vector.quantize_mx(out=x_codes[:, bags].bitcast(FP8X4), scales=x_scales[:, bags], in_=grouped[c][:])
+        multiply(0, [nc.vector.tensor_copy, nc.scalar.copy])
+        multiply(1, [nc.scalar.copy])
+        multiply(2, [nc.vector.tensor_copy])
+        multiply(3, [nc.scalar.copy, nc.vector.tensor_copy])

@@ -24,7 +24,7 @@ BANKS = 8
 TENSOR_CHUNK = 0
 MIXED_CHUNK = 1
 VECTOR_CHUNKS = (2, 3)
-EVEN_LOADS = (((0, 640), (640, 1024)), ((0, 384), (384, 768), (768, 1024)))
+EVEN_LOADS = (((0, 512), (512, 768), (768, 1024)), ((0, 512), (512, 1024)))
 
 
 def tile_picked_bag_lin_none_sub_l_kernel(tc, xT, w, gate, offs, out):
@@ -74,12 +74,12 @@ def tile_picked_bag_lin_none_sub_l_kernel(tc, xT, w, gate, offs, out):
         load_pair(1)
         nc.sync.dma_start(out=w_raw[:], in_=w.rearrange("(p t) m -> p t m", t=PACK))
 
-        def fill_low_halves(u, cast):
+        def fill_low_halves(u, casts):
             halves = pairs[u][:].bitcast(BF16).rearrange("p (i e) -> p i e", e=2)
-            for a, b in EVEN_LOADS[u]:
+            for (a, b), cast in zip(EVEN_LOADS[u], casts):
                 cast(halves[:, a:b, 0], even[u, a][:])
 
-        fill_low_halves(0, nc.vector.tensor_copy)
+        fill_low_halves(0, [nc.scalar.copy, nc.vector.tensor_copy, nc.vector.tensor_copy])
 
         gate_bank = take_bank("gate_bank", [P, CHUNKS, P])
         for c in range(CHUNKS):
@@ -88,7 +88,7 @@ def tile_picked_bag_lin_none_sub_l_kernel(tc, xT, w, gate, offs, out):
         nc.scalar.copy(gate_cols[:], gate_bank[:, :, 0 : D + 1])
         give_bank("gate_bank")
 
-        fill_low_halves(1, gpsimd_cast)
+        fill_low_halves(1, [nc.scalar.copy, gpsimd_cast])
 
         held = {d: take_bank("held%d" % d, [P, 2, 2, P]) for d in (1, 2)}
         turned = {}
@@ -140,9 +140,6 @@ def tile_picked_bag_lin_none_sub_l_kernel(tc, xT, w, gate, offs, out):
                 else:
                     dst = held[d][:, VECTOR_CHUNKS.index(c), u, :]
                 nc.tensor.transpose(dst, words[:, i * P : (i + 1) * P].bitcast(F32), ident[:])
-            for c in passing:
-                if d == 0 or c == TENSOR_CHUNK or u == 0:
-                    scale(u, d, c)
 
         def sum_back(acc, u):
             for e in range(2):
@@ -155,7 +152,7 @@ def tile_picked_bag_lin_none_sub_l_kernel(tc, xT, w, gate, offs, out):
             src, dst = (one_term, two_terms) if d == 1 else (two_terms, sums)
             values = held[d][:, VECTOR_CHUNKS.index(c), :, :].rearrange("v u p -> v (u p)").bitcast(BF16)
             nc.vector.scalar_tensor_tensor(dst[c][:], values, gate_cols[:, c, d : d + 1], src[c][:], MULT, ADD)
-            if c == VECTOR_CHUNKS[-1]:
+            if c == late:
                 give_bank("held%d" % d)
 
         def add_mixed(d, src, dst):
@@ -163,11 +160,11 @@ def tile_picked_bag_lin_none_sub_l_kernel(tc, xT, w, gate, offs, out):
             nc.vector.scalar_tensor_tensor(dst, values, gate_cols[:, MIXED_CHUNK, d : d + 1], src, MULT, ADD)
             was_read(1, d, MIXED_CHUNK)
 
-        def turn_back(c):
+        def turn_back(c, copy):
             bank = take_bank("back%d" % c, [P, 2, P])
             for u in (1, 0):
                 nc.tensor.transpose(bank[:, u, :], sums[c][:, pair_columns(u)].bitcast(F32), ident[:])
-            nc.scalar.copy(grouped[c][:].bitcast(F32).rearrange("p (v u) -> p v u", u=2), bank[:].rearrange("p u v -> p v u"))
+            copy(grouped[c][:].bitcast(F32).rearrange("p (v u) -> p v u", u=2), bank[:].rearrange("p u v -> p v u"))
             give_bank("back%d" % c)
 
         w_grouped = keep.tile([P, N, PACK], BF16, name="w_grouped", align_bytes=64)
@@ -176,6 +173,10 @@ def tile_picked_bag_lin_none_sub_l_kernel(tc, xT, w, gate, offs, out):
         x_codes = keep.tile([P, V], U32, name="x_codes", align_bytes=64)
         x_scales = keep.tile([P, V], U8, name="x_scales", align_bytes=64)
         out_rows = out.rearrange("(h p) v -> p h v", p=P)
+
+        def quantize(c):
+            bags = slice(c * P, (c + 1) * P)
+            nc.vector.quantize_mx(out=x_codes[:, bags].bitcast(FP8X4), scales=x_scales[:, bags], in_=grouped[c][:])
 
         def multiply(c, copies):
             bags = slice(c * P, (c + 1) * P)
@@ -202,36 +203,49 @@ def tile_picked_bag_lin_none_sub_l_kernel(tc, xT, w, gate, offs, out):
                 give_bank(name)
             nc.sync.dma_start(out=out_rows[:, :, bags], in_=result[:])
 
+        other_chunks = (TENSOR_CHUNK, MIXED_CHUNK)
+        late, early = VECTOR_CHUNKS
+
         for d in range(D):
-            gather(0, d, tuple(range(CHUNKS)))
+            gather(0, d, other_chunks + VECTOR_CHUNKS)
+            for c in other_chunks + VECTOR_CHUNKS if d == 0 else other_chunks:
+                scale(0, d, c)
+        gpsimd_cast(w_grouped[:], w_raw[:].rearrange("p t m -> p m t"))
         mixed_two = [keep.tile([P, 2 * P], F32, name="mixed_two%d" % u) for u in range(2)]
         nc.gpsimd.tensor_tensor(mixed_two[0][:], term[0, 0, MIXED_CHUNK][:], term[0, 1, MIXED_CHUNK][:], ADD)
-        gpsimd_cast(w_grouped[:], w_raw[:].rearrange("p t m -> p m t"))
         nc.gpsimd.tensor_tensor(sums[MIXED_CHUNK][:, pair_columns(0)], mixed_two[0][:], term[0, 2, MIXED_CHUNK][:], ADD)
         acc = take_bank("acc", [P, PACK, P])
         sum_back(acc, 0)
 
-        for d in range(D):
-            gather(1, d, (TENSOR_CHUNK, MIXED_CHUNK))
+        gather(1, 0, other_chunks)
+        for c in other_chunks:
+            scale(1, 0, c)
+        gather(1, 0, VECTOR_CHUNKS)
+        for d, c in ((1, early), (2, late)):
+            gather(1, d, other_chunks)
+            scale(1, d, TENSOR_CHUNK)
+            scale(1, 0, c)
+        for d in (1, 2):
             gather(1, d, VECTOR_CHUNKS)
         sum_back(acc, 1)
 
-        add_held(1, VECTOR_CHUNKS[0])
-        add_mixed(1, term[1, 0, MIXED_CHUNK][:], mixed_two[1][:])
-        add_held(1, VECTOR_CHUNKS[1])
-        add_mixed(2, mixed_two[1][:], sums[MIXED_CHUNK][:, pair_columns(1)])
-        for c in VECTOR_CHUNKS:
-            add_held(2, c)
-
         nc.vector.quantize_mx(out=w_codes[:].bitcast(FP8X4), scales=w_scales[:], in_=w_grouped[:].rearrange("p m t -> p (m t)"))
+        add_mixed(1, term[1, 0, MIXED_CHUNK][:], mixed_two[1][:])
+        add_held(1, early)
+        add_mixed(2, mixed_two[1][:], sums[MIXED_CHUNK][:, pair_columns(1)])
+        add_held(1, late)
+        add_held(2, early)
+
         nc.scalar.copy(grouped[TENSOR_CHUNK][:].rearrange("p (v t) -> p v t", t=PACK), acc[:].rearrange("p t v -> p v t"))
         give_bank("acc")
-        for c in (MIXED_CHUNK,) + VECTOR_CHUNKS:
-            turn_back(c)
-        for c in range(CHUNKS):
-            bags = slice(c * P, (c + 1) * P)
-            nc.vector.quantize_mx(out=x_codes[:, bags].bitcast(FP8X4), scales=x_scales[:, bags], in_=grouped[c][:])
-        multiply(0, [nc.vector.tensor_copy, nc.scalar.copy])
-        multiply(1, [nc.scalar.copy])
-        multiply(2, [nc.vector.tensor_copy])
-        multiply(3, [nc.scalar.copy, nc.vector.tensor_copy])
+        turn_back(MIXED_CHUNK, nc.scalar.copy)
+        turn_back(early, nc.scalar.copy)
+        quantize(TENSOR_CHUNK)
+        add_held(2, late)
+        turn_back(late, nc.vector.tensor_copy)
+        for c in (MIXED_CHUNK, early, late):
+            quantize(c)
+        multiply(TENSOR_CHUNK, [nc.vector.tensor_copy, nc.scalar.copy])
+        multiply(MIXED_CHUNK, [nc.vector.tensor_copy, nc.scalar.copy])
+        multiply(early, [nc.scalar.copy])
+        multiply(late, [nc.scalar.copy, nc.vector.tensor_copy])

from contextlib import ExitStack

import concourse.mybir as mybir
from concourse.masks import make_identity

K, T, D, V, N = 512, 1024, 3, 512, 256
FLOPS = 2 * K * V * N
BYTES = 4 * (K * T + K * N + D * V + N * V) + 2 * 128 * (D * V // 16)

F32 = mybir.dt.float32
BF16 = mybir.dt.bfloat16
U32 = mybir.dt.uint32
U16 = mybir.dt.uint16
U8 = mybir.dt.uint8
FP8X4 = mybir.dt.float8_e4m3fn_x4
COPY = mybir.ActivationFunctionType.Copy
MULT = mybir.AluOpType.mult
ADD = mybir.AluOpType.add

P = 128
PACK = 4
CHUNKS = V // P
BANKS = 8
TENSOR_CHUNK = 0
MIXED_CHUNK = 1
VECTOR_CHUNKS = (2, 3)
EVEN_LOADS = (((0, 512), (512, 768), (768, 1024)), ((0, 512), (512, 1024)))


def tile_picked_bag_lin_none_sub_l_kernel(tc, xT, w, gate, offs, out):
    nc = tc.nc
    with ExitStack() as ctx:
        keep = ctx.enter_context(tc.tile_pool(name="keep", bufs=1))
        psum = ctx.enter_context(tc.psum_pool(name="psum", bufs=1))

        free_banks = list(range(BANKS))
        bank_number = {}

        def take_bank(name, shape):
            bank_number[name] = free_banks.pop(0)
            return psum.tile(shape, F32, tag="bank%d" % bank_number[name], name=name)

        def give_bank(name):
            free_banks.append(bank_number[name])

        def gpsimd_cast(dst, src):
            nc.gpsimd.tensor_scalar(dst, src, 1.0, 0.0, MULT, ADD)

        offsets = keep.tile([P, D * V // 16], U16, name="offsets")
        x_rows = xT.rearrange("(p t) i -> p t i", t=PACK)
        pairs = [keep.tile([P, T], F32, name="pairs%d" % u, align_bytes=64) for u in range(2)]
        even = {}
        for u in range(2):
            for a, b in EVEN_LOADS[u]:
                even[u, a] = keep.tile([P, b - a], F32, name="even%d_%d" % (u, a))
        gate_rows = keep.tile([P, V], F32, name="gate_rows")
        w_raw = keep.tile([P, PACK, N], F32, name="w_raw")
        ident = keep.tile([P, P], F32, name="ident")
        warm = keep.tile([P, 8], F32, name="warm")

        nc.gpsimd.memset(gate_rows[:], 0.0)
        make_identity(nc, ident[:])
        nc.vector.memset(warm[:], 0.0)
        nc.scalar.activation(warm[:, 4:8], warm[:, 0:4], COPY, scale=warm[:, 0:1])

        def load_pair(u):
            nc.sync.dma_start(out=pairs[u][:], in_=x_rows[:, 2 * u + 1, :])
            for a, b in EVEN_LOADS[u]:
                nc.sync.dma_start(out=even[u, a][:], in_=x_rows[:, 2 * u, a:b])

        load_pair(0)
        nc.sync.dma_start(offsets[:], offs)
        nc.sync.dma_start(out=gate_rows[0:D, :], in_=gate[:, 0, :])
        load_pair(1)
        nc.sync.dma_start(out=w_raw[:], in_=w.rearrange("(p t) m -> p t m", t=PACK))

        def fill_low_halves(u, casts):
            halves = pairs[u][:].bitcast(BF16).rearrange("p (i e) -> p i e", e=2)
            for (a, b), cast in zip(EVEN_LOADS[u], casts):
                cast(halves[:, a:b, 0], even[u, a][:])

        fill_low_halves(0, [nc.scalar.copy, nc.vector.tensor_copy, nc.vector.tensor_copy])

        gate_bank = take_bank("gate_bank", [P, CHUNKS, P])
        for c in range(CHUNKS):
            nc.tensor.transpose(gate_bank[:, c, :], gate_rows[:, c * P : (c + 1) * P], ident[:])
        gate_cols = keep.tile([P, CHUNKS, D + 1], F32, name="gate_cols")
        nc.scalar.copy(gate_cols[:], gate_bank[:, :, 0 : D + 1])
        give_bank("gate_bank")

        fill_low_halves(1, [nc.scalar.copy, gpsimd_cast])

        held = {d: take_bank("held%d" % d, [P, 2, 2, P]) for d in (1, 2)}
        turned = {}
        turned_in = {}
        readers_left = {}
        term = {}
        one_term = {c: keep.tile([P, K], F32, name="one_term%d" % c) for c in VECTOR_CHUNKS}
        two_terms = {c: keep.tile([P, K], F32, name="two_terms%d" % c) for c in VECTOR_CHUNKS}
        sums = {c: keep.tile([P, K], BF16, name="sums%d" % c) for c in (MIXED_CHUNK,) + VECTOR_CHUNKS}
        grouped = [keep.tile([P, PACK * P], BF16, name="grouped%d" % c, align_bytes=64) for c in range(CHUNKS)]

        def pair_columns(u):
            return slice(2 * P * u, 2 * P * (u + 1))

        def was_read(u, d, c):
            readers_left[turned_in[u, d, c]] -= 1
            if readers_left[turned_in[u, d, c]] == 0:
                give_bank(turned_in[u, d, c])

        def scale(u, d, c):
            values = turned[u, d, c].bitcast(BF16)
            if c in VECTOR_CHUNKS:
                dst = one_term[c][:, pair_columns(u)]
            elif c == MIXED_CHUNK:
                term[u, d, c] = keep.tile([P, 2 * P], F32, name="term%d%d%d" % (u, d, c))
                dst = term[u, d, c][:]
            else:
                term[u, d, c] = keep.tile([P, 2, P], F32, name="term%d%d%d" % (u, d, c))
                dst = term[u, d, c][:]
                values = values.rearrange("v (p e) -> v e p", e=2)
            nc.scalar.activation(dst, values, COPY, scale=gate_cols[:, c, d : d + 1])
            was_read(u, d, c)

        def gather(u, d, chunks):
            n = len(chunks) * P
            first = d * V + chunks[0] * P
            words = keep.tile([P, n], U32, name="words%d%d%d" % (u, d, chunks[0]))
            nc.vector.tensor_copy(words[:], pairs[u][:].bitcast(U32).indirect(offsets[:, first // 16 : (first + n) // 16]))
            passing = [c for c in chunks if d == 0 or c not in VECTOR_CHUNKS]
            if passing:
                name = "turned%d%d%d" % (u, d, chunks[0])
                bank = take_bank(name, [P, CHUNKS, P])
                readers_left[name] = len(passing)
            for i, c in enumerate(chunks):
                if c in passing:
                    turned[u, d, c] = bank[:, i, :]
                    turned_in[u, d, c] = name
                    dst = turned[u, d, c]
                else:
                    dst = held[d][:, VECTOR_CHUNKS.index(c), u, :]
                nc.tensor.transpose(dst, words[:, i * P : (i + 1) * P].bitcast(F32), ident[:])

        def sum_back(acc, u):
            for e in range(2):
                for d in range(D):
                    nc.tensor.matmul(
                        acc[:, 2 * u + e, :], term[u, d, TENSOR_CHUNK][:, e, :], ident[:], start=(d == 0), stop=(d == D - 1), is_transpose=True
                    )

        def add_held(d, c):
            src, dst = (one_term, two_terms) if d == 1 else (two_terms, sums)
            values = held[d][:, VECTOR_CHUNKS.index(c), :, :].rearrange("v u p -> v (u p)").bitcast(BF16)
            nc.vector.scalar_tensor_tensor(dst[c][:], values, gate_cols[:, c, d : d + 1], src[c][:], MULT, ADD)
            if c == late:
                give_bank("held%d" % d)

        def add_mixed(d, src, dst):
            values = turned[1, d, MIXED_CHUNK].bitcast(BF16)
            nc.vector.scalar_tensor_tensor(dst, values, gate_cols[:, MIXED_CHUNK, d : d + 1], src, MULT, ADD)
            was_read(1, d, MIXED_CHUNK)

        def turn_back(c, copy):
            bank = take_bank("back%d" % c, [P, 2, P])
            for u in (1, 0):
                nc.tensor.transpose(bank[:, u, :], sums[c][:, pair_columns(u)].bitcast(F32), ident[:])
            copy(grouped[c][:].bitcast(F32).rearrange("p (v u) -> p v u", u=2), bank[:].rearrange("p u v -> p v u"))
            give_bank("back%d" % c)

        w_grouped = keep.tile([P, N, PACK], BF16, name="w_grouped", align_bytes=64)
        w_codes = keep.tile([P, N], U32, name="w_codes", align_bytes=64)
        w_scales = keep.tile([P, N], U8, name="w_scales", align_bytes=64)
        x_codes = keep.tile([P, V], U32, name="x_codes", align_bytes=64)
        x_scales = keep.tile([P, V], U8, name="x_scales", align_bytes=64)
        out_rows = out.rearrange("(h p) v -> p h v", p=P)

        def quantize(c):
            bags = slice(c * P, (c + 1) * P)
            nc.vector.quantize_mx(out=x_codes[:, bags].bitcast(FP8X4), scales=x_scales[:, bags], in_=grouped[c][:])

        def multiply(c, copies):
            bags = slice(c * P, (c + 1) * P)
            result = keep.tile([P, 2, P], F32, name="result%d" % c)
            names = ["product%d%d" % (c, i) for i in range(len(copies))]
            banks = [take_bank(name, [P, 2, P]) for name in names]
            for h in range(2):
                rows = slice(h * P, (h + 1) * P)
                nc.tensor.matmul_mx(
                    out=banks[h % len(copies)][:, h, :],
                    lhsT=w_codes[:, rows].bitcast(FP8X4),
                    lhsT_scale=w_scales[:, rows],
                    rhs=x_codes[:, bags].bitcast(FP8X4),
                    rhs_scale=x_scales[:, bags],
                    start=True,
                    stop=True,
                )
            if len(copies) == 1:
                copies[0](result[:], banks[0][:])
            else:
                for h in range(2):
                    copies[h](result[:, h, :], banks[h][:, h, :])
            for name in names:
                give_bank(name)
            nc.sync.dma_start(out=out_rows[:, :, bags], in_=result[:])

        other_chunks = (TENSOR_CHUNK, MIXED_CHUNK)
        late, early = VECTOR_CHUNKS

        for d in range(D):
            gather(0, d, other_chunks + VECTOR_CHUNKS)
            for c in other_chunks + VECTOR_CHUNKS if d == 0 else other_chunks:
                scale(0, d, c)
        gpsimd_cast(w_grouped[:], w_raw[:].rearrange("p t m -> p m t"))
        mixed_two = [keep.tile([P, 2 * P], F32, name="mixed_two%d" % u) for u in range(2)]
        nc.gpsimd.tensor_tensor(mixed_two[0][:], term[0, 0, MIXED_CHUNK][:], term[0, 1, MIXED_CHUNK][:], ADD)
        nc.gpsimd.tensor_tensor(sums[MIXED_CHUNK][:, pair_columns(0)], mixed_two[0][:], term[0, 2, MIXED_CHUNK][:], ADD)
        acc = take_bank("acc", [P, PACK, P])
        sum_back(acc, 0)

        gather(1, 0, other_chunks)
        for c in other_chunks:
            scale(1, 0, c)
        gather(1, 0, VECTOR_CHUNKS)
        for d, c in ((1, early), (2, late)):
            gather(1, d, other_chunks)
            scale(1, d, TENSOR_CHUNK)
            scale(1, 0, c)
        for d in (1, 2):
            gather(1, d, VECTOR_CHUNKS)
        sum_back(acc, 1)

        nc.vector.quantize_mx(out=w_codes[:].bitcast(FP8X4), scales=w_scales[:], in_=w_grouped[:].rearrange("p m t -> p (m t)"))
        add_mixed(1, term[1, 0, MIXED_CHUNK][:], mixed_two[1][:])
        add_held(1, early)
        add_mixed(2, mixed_two[1][:], sums[MIXED_CHUNK][:, pair_columns(1)])
        add_held(1, late)
        add_held(2, early)

        nc.scalar.copy(grouped[TENSOR_CHUNK][:].rearrange("p (v t) -> p v t", t=PACK), acc[:].rearrange("p t v -> p v t"))
        give_bank("acc")
        turn_back(MIXED_CHUNK, nc.scalar.copy)
        turn_back(early, nc.scalar.copy)
        quantize(TENSOR_CHUNK)
        add_held(2, late)
        turn_back(late, nc.vector.tensor_copy)
        for c in (MIXED_CHUNK, early, late):
            quantize(c)
        multiply(TENSOR_CHUNK, [nc.vector.tensor_copy, nc.scalar.copy])
        multiply(MIXED_CHUNK, [nc.vector.tensor_copy, nc.scalar.copy])
        multiply(early, [nc.scalar.copy])
        multiply(late, [nc.scalar.copy, nc.vector.tensor_copy])
